import numpy as np
import ml_dtypes

BF16 = ml_dtypes.bfloat16


def bf(x):
    return np.asarray(x, np.float32).astype(BF16)


def f32(x):
    return np.asarray(x, np.float32)


def f64(x):
    return np.asarray(x).astype(np.float64)


def striped(idx):
    return np.concatenate([l.reshape(-1, 16).T for l in idx])


def rows(idx, k):
    return np.tile(np.repeat(idx, 16, axis=0), (k // (16 * 8), 1))


def look(tab, idx):
    return np.take_along_axis(f64(tab), rows(idx, len(tab)), axis=1)


K, S, D, V, N = 128, 2048, 3, 512, 1536


def setup_inputs():
    return {"tab": f32(np.random.standard_normal((K, S))), "x0": f32(np.random.standard_normal((K, V))), "offs": striped(np.stack([np.random.permutation(S)[:N] for _ in range(8)]))}


def reference(tab, x0, offs):
    idx = np.stack([g.T.reshape(-1) for g in np.split(offs, 8)])
    x = f64(x0)
    for d in range(D):
        x = np.minimum(x, look(tab, idx[:, d * V:(d + 1) * V]))
    return x

@@ -1,0 +1,23 @@
+import concourse.mybir as mybir
+
+F32, U16 = mybir.dt.float32, mybir.dt.uint16
+MIN = mybir.AluOpType.min
+ROWS, TABLE_COLS, D, V = 128, 2048, 3, 512
+LIST_COLS = V // 16
+
+def tile_lookup_pool_min_out_kernel(tc, tab, x0, offs, out):
+    nc = tc.nc
+    with tc.tile_pool(name="held", bufs=1) as held:
+        offsets = held.tile([ROWS, D * LIST_COLS], U16, name="offsets")
+        table = held.tile([ROWS, TABLE_COLS], F32, name="table")
+        x = [held.tile([ROWS, V], F32, name=f"x{d}") for d in range(D + 1)]
+
+        nc.sync.dma_start(table[:], tab)
+        nc.sync.dma_start(offsets[:], offs)
+        nc.scalar.dma_start(x[0][:], x0)
+
+        for d in range(D):
+            piece = offsets[:, d * LIST_COLS : (d + 1) * LIST_COLS]
+            nc.vector.tensor_tensor(x[d + 1][:], table[:].indirect(piece), x[d][:], MIN)
+
+        nc.sync.dma_start(out, x[D][:])

@@ -5,6 +5,7 @@ MIN = mybir.AluOpType.min
 ROWS, TABLE_COLS, D, V = 128, 2048, 3, 512
 LIST_COLS = V // 16
 
+
 def tile_lookup_pool_min_out_kernel(tc, tab, x0, offs, out):
     nc = tc.nc
     with tc.tile_pool(name="held", bufs=1) as held:
@@ -14,7 +15,7 @@ def tile_lookup_pool_min_out_kernel(tc, tab, x0, offs, out):
 
         nc.sync.dma_start(table[:], tab)
         nc.sync.dma_start(offsets[:], offs)
-        nc.scalar.dma_start(x[0][:], x0)
+        nc.sync.dma_start(x[0][:], x0)
 
         for d in range(D):
             piece = offsets[:, d * LIST_COLS : (d + 1) * LIST_COLS]

@@ -4,14 +4,15 @@ F32, U16 = mybir.dt.float32, mybir.dt.uint16
 MIN = mybir.AluOpType.min
 ROWS, TABLE_COLS, D, V = 128, 2048, 3, 512
 LIST_COLS = V // 16
+ALIGN = 512
 
 
 def tile_lookup_pool_min_out_kernel(tc, tab, x0, offs, out):
     nc = tc.nc
     with tc.tile_pool(name="held", bufs=1) as held:
-        offsets = held.tile([ROWS, D * LIST_COLS], U16, name="offsets")
-        table = held.tile([ROWS, TABLE_COLS], F32, name="table")
-        x = [held.tile([ROWS, V], F32, name=f"x{d}") for d in range(D + 1)]
+        offsets = held.tile([ROWS, D * LIST_COLS], U16, name="offsets", align_bytes=ALIGN)
+        table = held.tile([ROWS, TABLE_COLS], F32, name="table", align_bytes=ALIGN)
+        x = [held.tile([ROWS, V], F32, name=f"x{d}", align_bytes=ALIGN) for d in range(D + 1)]
 
         nc.sync.dma_start(table[:], tab)
         nc.sync.dma_start(offsets[:], offs)

@@ -4,7 +4,7 @@ F32, U16 = mybir.dt.float32, mybir.dt.uint16
 MIN = mybir.AluOpType.min
 ROWS, TABLE_COLS, D, V = 128, 2048, 3, 512
 LIST_COLS = V // 16
-ALIGN = 512
+ALIGN = 4096
 
 
 def tile_lookup_pool_min_out_kernel(tc, tab, x0, offs, out):

@@ -5,14 +5,16 @@ MIN = mybir.AluOpType.min
 ROWS, TABLE_COLS, D, V = 128, 2048, 3, 512
 LIST_COLS = V // 16
 ALIGN = 4096
+ORIGIN_ALIGN = 65536
+TABLE_AT = ORIGIN_ALIGN - TABLE_COLS * 4 // 2
 
 
 def tile_lookup_pool_min_out_kernel(tc, tab, x0, offs, out):
     nc = tc.nc
     with tc.tile_pool(name="held", bufs=1) as held:
-        offsets = held.tile([ROWS, D * LIST_COLS], U16, name="offsets", align_bytes=ALIGN)
-        table = held.tile([ROWS, TABLE_COLS], F32, name="table", align_bytes=ALIGN)
-        x = [held.tile([ROWS, V], F32, name=f"x{d}", align_bytes=ALIGN) for d in range(D + 1)]
+        offsets = held.tile([ROWS, D * LIST_COLS], U16, name="offsets", align_bytes=ORIGIN_ALIGN, offset=0)
+        table = held.tile([ROWS, TABLE_COLS], F32, name="table", align_bytes=ALIGN, offset=TABLE_AT)
+        x = [held.tile([ROWS, V], F32, name=f"x{d}", align_bytes=ALIGN, offset=(d + 1) * ALIGN) for d in range(D + 1)]
 
         nc.sync.dma_start(table[:], tab)
         nc.sync.dma_start(offsets[:], offs)

@@ -4,6 +4,7 @@ F32, U16 = mybir.dt.float32, mybir.dt.uint16
 MIN = mybir.AluOpType.min
 ROWS, TABLE_COLS, D, V = 128, 2048, 3, 512
 LIST_COLS = V // 16
+WARM_COLS = 16
 ALIGN = 4096
 ORIGIN_ALIGN = 65536
 TABLE_AT = ORIGIN_ALIGN - TABLE_COLS * 4 // 2
@@ -16,9 +17,14 @@ def tile_lookup_pool_min_out_kernel(tc, tab, x0, offs, out):
         table = held.tile([ROWS, TABLE_COLS], F32, name="table", align_bytes=ALIGN, offset=TABLE_AT)
         x = [held.tile([ROWS, V], F32, name=f"x{d}", align_bytes=ALIGN, offset=(d + 1) * ALIGN) for d in range(D + 1)]
 
+        scratch = [held.tile([ROWS, WARM_COLS], F32, name=f"scratch{i}", offset=(D + 2 + i) * ALIGN) for i in range(2)]
+
         nc.sync.dma_start(table[:], tab)
-        nc.sync.dma_start(offsets[:], offs)
         nc.sync.dma_start(x[0][:], x0)
+        nc.sync.dma_start(offsets[:], offs)
+
+        nc.vector.tensor_copy(scratch[0][:], table[:, :WARM_COLS])
+        nc.vector.tensor_copy(scratch[1][:], x[0][:, :WARM_COLS])
 
         for d in range(D):
             piece = offsets[:, d * LIST_COLS : (d + 1) * LIST_COLS]

@@ -6,18 +6,15 @@ ROWS, TABLE_COLS, D, V = 128, 2048, 3, 512
 LIST_COLS = V // 16
 WARM_COLS = 16
 ALIGN = 4096
-ORIGIN_ALIGN = 65536
-TABLE_AT = ORIGIN_ALIGN - TABLE_COLS * 4 // 2
 
 
 def tile_lookup_pool_min_out_kernel(tc, tab, x0, offs, out):
     nc = tc.nc
     with tc.tile_pool(name="held", bufs=1) as held:
-        offsets = held.tile([ROWS, D * LIST_COLS], U16, name="offsets", align_bytes=ORIGIN_ALIGN, offset=0)
-        table = held.tile([ROWS, TABLE_COLS], F32, name="table", align_bytes=ALIGN, offset=TABLE_AT)
-        x = [held.tile([ROWS, V], F32, name=f"x{d}", align_bytes=ALIGN, offset=(d + 1) * ALIGN) for d in range(D + 1)]
-
-        scratch = [held.tile([ROWS, WARM_COLS], F32, name=f"scratch{i}", offset=(D + 2 + i) * ALIGN) for i in range(2)]
+        offsets = held.tile([ROWS, D * LIST_COLS], U16, name="offsets", align_bytes=ALIGN)
+        table = held.tile([ROWS, TABLE_COLS], F32, name="table", align_bytes=ALIGN)
+        x = [held.tile([ROWS, V], F32, name=f"x{i}", align_bytes=ALIGN) for i in range(2)]
+        scratch = [held.tile([ROWS, WARM_COLS], F32, name=f"scratch{i}") for i in range(2)]
 
         nc.sync.dma_start(table[:], tab)
         nc.sync.dma_start(x[0][:], x0)
@@ -28,6 +25,6 @@ def tile_lookup_pool_min_out_kernel(tc, tab, x0, offs, out):
 
         for d in range(D):
             piece = offsets[:, d * LIST_COLS : (d + 1) * LIST_COLS]
-            nc.vector.tensor_tensor(x[d + 1][:], table[:].indirect(piece), x[d][:], MIN)
+            nc.vector.tensor_tensor(x[(d + 1) % 2][:], table[:].indirect(piece), x[d % 2][:], MIN)
 
-        nc.sync.dma_start(out, x[D][:])
+        nc.sync.dma_start(out, x[D % 2][:])

@@ -16,12 +16,12 @@ def tile_lookup_pool_min_out_kernel(tc, tab, x0, offs, out):
         x = [held.tile([ROWS, V], F32, name=f"x{i}", align_bytes=ALIGN) for i in range(2)]
         scratch = [held.tile([ROWS, WARM_COLS], F32, name=f"scratch{i}") for i in range(2)]
 
-        nc.sync.dma_start(table[:], tab)
         nc.sync.dma_start(x[0][:], x0)
+        nc.sync.dma_start(table[:], tab)
         nc.sync.dma_start(offsets[:], offs)
 
-        nc.vector.tensor_copy(scratch[0][:], table[:, :WARM_COLS])
-        nc.vector.tensor_copy(scratch[1][:], x[0][:, :WARM_COLS])
+        nc.vector.tensor_copy(scratch[0][:], x[0][:, :WARM_COLS])
+        nc.vector.tensor_copy(scratch[1][:], table[:, :WARM_COLS])
 
         for d in range(D):
             piece = offsets[:, d * LIST_COLS : (d + 1) * LIST_COLS]

@@ -16,8 +16,8 @@ def tile_lookup_pool_min_out_kernel(tc, tab, x0, offs, out):
         x = [held.tile([ROWS, V], F32, name=f"x{i}", align_bytes=ALIGN) for i in range(2)]
         scratch = [held.tile([ROWS, WARM_COLS], F32, name=f"scratch{i}") for i in range(2)]
 
-        nc.sync.dma_start(x[0][:], x0)
-        nc.sync.dma_start(table[:], tab)
+        nc.scalar.dma_start(x[0][:], x0)
+        nc.scalar.dma_start(table[:], tab)
         nc.sync.dma_start(offsets[:], offs)
 
         nc.vector.tensor_copy(scratch[0][:], x[0][:, :WARM_COLS])

@@ -16,9 +16,9 @@ def tile_lookup_pool_min_out_kernel(tc, tab, x0, offs, out):
         x = [held.tile([ROWS, V], F32, name=f"x{i}", align_bytes=ALIGN) for i in range(2)]
         scratch = [held.tile([ROWS, WARM_COLS], F32, name=f"scratch{i}") for i in range(2)]
 
-        nc.scalar.dma_start(x[0][:], x0)
-        nc.scalar.dma_start(table[:], tab)
+        nc.sync.dma_start(x[0][:], x0)
         nc.sync.dma_start(offsets[:], offs)
+        nc.scalar.dma_start(table[:], tab)
 
         nc.vector.tensor_copy(scratch[0][:], x[0][:, :WARM_COLS])
         nc.vector.tensor_copy(scratch[1][:], table[:, :WARM_COLS])
@@ -27,4 +27,4 @@ def tile_lookup_pool_min_out_kernel(tc, tab, x0, offs, out):
             piece = offsets[:, d * LIST_COLS : (d + 1) * LIST_COLS]
             nc.vector.tensor_tensor(x[(d + 1) % 2][:], table[:].indirect(piece), x[d % 2][:], MIN)
 
-        nc.sync.dma_start(out, x[D % 2][:])
+        nc.scalar.dma_start(out, x[D % 2][:])

import concourse.mybir as mybir

F32, U16 = mybir.dt.float32, mybir.dt.uint16
MIN = mybir.AluOpType.min
ROWS, TABLE_COLS, D, V = 128, 2048, 3, 512
LIST_COLS = V // 16
WARM_COLS = 16
ALIGN = 4096


def tile_lookup_pool_min_out_kernel(tc, tab, x0, offs, out):
    nc = tc.nc
    with tc.tile_pool(name="held", bufs=1) as held:
        offsets = held.tile([ROWS, D * LIST_COLS], U16, name="offsets", align_bytes=ALIGN)
        table = held.tile([ROWS, TABLE_COLS], F32, name="table", align_bytes=ALIGN)
        x = [held.tile([ROWS, V], F32, name=f"x{i}", align_bytes=ALIGN) for i in range(2)]
        scratch = [held.tile([ROWS, WARM_COLS], F32, name=f"scratch{i}") for i in range(2)]

        nc.sync.dma_start(x[0][:], x0)
        nc.sync.dma_start(offsets[:], offs)
        nc.scalar.dma_start(table[:], tab)

        nc.vector.tensor_copy(scratch[0][:], x[0][:, :WARM_COLS])
        nc.vector.tensor_copy(scratch[1][:], table[:, :WARM_COLS])

        for d in range(D):
            piece = offsets[:, d * LIST_COLS : (d + 1) * LIST_COLS]
            nc.vector.tensor_tensor(x[(d + 1) % 2][:], table[:].indirect(piece), x[d % 2][:], MIN)

        nc.scalar.dma_start(out, x[D % 2][:])
